import numpy as np
import ml_dtypes


def mxq(x, axis, fmt="e4m3"):
    dtype, down = {"e4m3": (ml_dtypes.float8_e4m3fn, 7), "e5m2": (ml_dtypes.float8_e5m2, 14)}[fmt]
    v = np.moveaxis(np.asarray(x, np.float32).astype(ml_dtypes.bfloat16).astype(np.float64), axis, -1)
    blocks = v.reshape(v.shape[:-1] + (-1, 32))
    amax = np.abs(blocks).max(-1, keepdims=True)
    byte = np.maximum(np.where(amax > 0, np.frexp(amax)[1] - 1 + 127, 0) - down, 1)
    scale = np.exp2(byte - 127.0)
    codes = (blocks / scale).astype(np.float32).astype(dtype).astype(np.float64)
    return np.moveaxis((codes * scale).reshape(v.shape), -1, axis)


WIDE = False


def mx_kscale(k):
    if not WIDE:
        return np.ones(k)
    levels = np.array([10, -10, 5, -5, 0])
    if k % 512:
        return np.exp2(np.random.permutation(np.resize(levels, k // 32))).repeat(32)
    a = np.empty((k // 512, 16))
    for p in range(k // 512):
        a[p, :8] = np.random.permutation(np.resize(levels, 8))
        for g in range(8):
            far = levels[np.abs(levels - a[p, g]) >= 10]
            a[p, g + 8] = far[np.random.randint(len(far))]
    return np.exp2(a.ravel()).repeat(32)


def f64(x):
    return np.asarray(x).astype(np.float64)


def striped(idx):
    return np.tile(idx.reshape(-1, 16).T, (8, 1)).astype(np.uint16)


def unstriped(offs):
    return offs[:16].T.reshape(-1).astype(np.int64)


def relu2(v):
    return np.maximum(v, 0.0) ** 2


K, T, S, N = 2048, 1024, 512, 128


def setup_inputs():
    n = np.random.standard_normal
    s = mx_kscale(K)[:, None]
    return {
        "xT": (n((K, S)) * s).astype(np.float32),
        "w": (n((K, N)) / np.sqrt(K) / s).astype(np.float32),
        "b": (0.3 * n((N, 1))).astype(np.float32),
        "gate": np.tile(np.random.uniform(0.2, 1.0, S), (N, 1)).astype(np.float32),
        "offs": striped(np.random.permutation(T)[:S]),
    }


def reference(xT, w, b, gate, offs):
    idx = unstriped(offs)
    xq = mxq(f64(xT), 0, "e4m3")
    y = mxq(f64(w), 0, "e4m3").T @ xq
    y = relu2(y + f64(b))
    out = np.zeros((N, T))
    out[:, idx] = f64(gate) * y
    return out

@@ -1,0 +1,162 @@
+from contextlib import ExitStack
+
+import concourse.mybir as mybir
+
+K, T, S, N = 2048, 1024, 512, 128
+P = 128
+PACK = 4
+K_PASS = P * PACK
+PASSES = K // K_PASS
+FLOPS = 2 * K * S * N
+
+F32 = mybir.dt.float32
+BF16 = mybir.dt.bfloat16
+U32 = mybir.dt.uint32
+U16 = mybir.dt.uint16
+U8 = mybir.dt.uint8
+FP8X4 = mybir.dt.float8_e4m3fn_x4
+MULT = mybir.AluOpType.mult
+RELU = mybir.ActivationFunctionType.Relu
+SQUARE = mybir.ActivationFunctionType.Square
+
+STEPS = (
+    ("w", 0, 2, 0, 128, 48),
+    ("small", 0, 0, 0, 0, 0),
+    ("w", 2, 4, 0, 128, 48),
+    ("x", 0, 1, 0, 256, 96),
+    ("x", 1, 2, 0, 256, 112),
+    ("x", 2, 3, 0, 128, 64),
+    ("x", 3, 4, 0, 128, 128),
+    ("x", 2, 3, 128, 256, 56),
+    ("x", 3, 4, 128, 256, 72),
+    ("x", 2, 3, 256, 384, 56),
+    ("gate", 0, 0, 0, 512, 0),
+    ("x", 0, 2, 256, 384, 128),
+    ("x", 3, 4, 256, 512, 96),
+    ("x", 0, 1, 384, 512, 128),
+    ("x", 1, 2, 384, 512, 128),
+    ("x", 2, 3, 384, 512, 0),
+)
+GROUPS = ((0, 128), (128, 256), (256, 384), (384, 512))
+SCATTER = 128
+
+
+def tile_picked_place_lin_relu2_sub_l_kernel(tc, xT, w, b, gate, offs, out):
+    nc = tc.nc
+    with ExitStack() as ctx:
+        keep = ctx.enter_context(tc.tile_pool(name="keep", bufs=1))
+        psum = ctx.enter_context(tc.psum_pool(name="psum", bufs=1))
+
+        offsets = keep.tile([P, S // 16], U16, name="offsets")
+        bias = keep.tile([P, 1], F32, name="bias")
+        gates = keep.tile([P, S], F32, name="gates")
+        warm = keep.tile([P, 8], F32, name="warm")
+        window = keep.tile([P, T], F32, name="window")
+        accs = [psum.tile([P, hi - lo], F32, name=f"acc{lo}") for lo, hi in GROUPS]
+
+        w_view = w.rearrange("(c p j) n -> c p j n", p=P, j=PACK)
+        x_view = xT.rearrange("(c p j) s -> c p j s", p=P, j=PACK)
+        raws = {}
+        for n, (what, c_lo, c_hi, lo, hi, share) in enumerate(STEPS):
+            if what == "small":
+                nc.sync.dma_start(offsets[:], offs)
+                nc.sync.dma_start(out=bias[:], in_=b)
+            elif what == "gate":
+                nc.sync.dma_start(out=gates[:, lo:hi], in_=gate[:, lo:hi])
+            else:
+                view = w_view if what == "w" else x_view
+                raw = keep.tile([P, c_hi - c_lo, PACK, hi - lo], F32, name=f"raw_{what}{c_lo}_{lo}")
+                for c in range(c_lo, c_hi):
+                    nc.sync.dma_start(out=raw[:, c - c_lo], in_=view[c, :, :, lo:hi])
+                raws[n] = raw
+
+        nc.vector.memset(warm[:], 0.0)
+        nc.scalar.activation(out=warm[:, 0:1], in_=warm[:, 1:2], func=RELU)
+        nc.gpsimd.memset(window[:], 0.0)
+
+        w_parts = {}
+        x_parts = {}
+
+        def quantize(n):
+            what, c_lo, c_hi, lo, hi, share = STEPS[n]
+            raw = raws[n]
+            width = hi - lo
+            passes = c_hi - c_lo
+            grouped = keep.tile([P, passes, width, PACK], BF16, name=f"grouped_{what}{c_lo}_{lo}", align_bytes=64)
+            codes = keep.tile([P, passes * width], U32, name=f"codes_{what}{c_lo}_{lo}", align_bytes=64)
+            scales = keep.tile([P, passes * width], U8, name=f"scales_{what}{c_lo}_{lo}", align_bytes=64)
+            for copy, a, b in ((nc.scalar.copy, 0, share), (nc.vector.tensor_copy, share, width)):
+                if a == b:
+                    continue
+                if passes == 1:
+                    copy(
+                        out=grouped[:, 0, a:b].rearrange("p (s i) j -> p s j i", i=4),
+                        in_=raw[:, 0, :, a:b].rearrange("p j (s i) -> p s j i", i=4),
+                    )
+                else:
+                    copy(out=grouped[:, :, a:b], in_=raw[:, :, :, a:b].rearrange("p c j s -> p c s j"))
+            nc.vector.quantize_mx(
+                out=codes[:].bitcast(FP8X4), scales=scales[:], in_=grouped[:].rearrange("p c s j -> p (c s j)")
+            )
+            for c in range(c_lo, c_hi):
+                part = (codes, scales, (c - c_lo) * width)
+                if what == "w":
+                    w_parts[c] = part
+                else:
+                    x_parts[(c, lo)] = part
+
+        products = [0] * len(GROUPS)
+
+        def multiply(c, x_lo, g):
+            lo, hi = GROUPS[g]
+            w_codes, w_scales, w_at = w_parts[c]
+            x_codes, x_scales, x_at = x_parts[(c, x_lo)]
+            w_cols = slice(w_at, w_at + N)
+            x_cols = slice(x_at + lo - x_lo, x_at + hi - x_lo)
+            nc.tensor.matmul_mx(
+                out=accs[g][:],
+                lhsT=w_codes[:, w_cols].bitcast(FP8X4),
+                lhsT_scale=w_scales[:, w_cols],
+                rhs=x_codes[:, x_cols].bitcast(FP8X4),
+                rhs_scale=x_scales[:, x_cols],
+                start=(products[g] == 0),
+                stop=(products[g] == PASSES - 1),
+            )
+            products[g] += 1
+
+        pending = []
+
+        def activate(g):
+            lo, hi = GROUPS[g]
+            relu = keep.tile([P, hi - lo], F32, name=f"relu_{lo}")
+            relu2 = keep.tile([P, hi - lo], F32, name=f"relu2_{lo}")
+            nc.scalar.activation(out=relu[:], in_=accs[g][:], func=RELU, bias=bias[:])
+            nc.scalar.activation(out=relu2[:], in_=relu[:], func=SQUARE)
+            for q in range(lo, hi, SCATTER):
+                pending.append((relu2[:, q - lo : q - lo + SCATTER], q, q + SCATTER))
+
+        def scatter_one():
+            relu2, lo, hi = pending.pop(0)
+            nc.vector.tensor_tensor(
+                window[:].indirect(offsets[:, lo // 16 : hi // 16]), relu2, gates[:, lo:hi], MULT
+            )
+
+        waiting = []
+        for n, (what, c_lo, c_hi, lo, hi, share) in enumerate(STEPS):
+            if what in ("small", "gate"):
+                continue
+            quantize(n)
+            if pending:
+                scatter_one()
+            if what == "x":
+                waiting.extend((c, lo, g) for c in range(c_lo, c_hi) for g in range(len(GROUPS)) if lo <= GROUPS[g][0] < hi)
+            ready = [item for item in waiting if item[0] in w_parts]
+            waiting = [item for item in waiting if item[0] not in w_parts]
+            for c, x_lo, g in ready:
+                multiply(c, x_lo, g)
+                if products[g] == PASSES:
+                    activate(g)
+        while pending:
+            scatter_one()
+
+        nc.sync.dma_start(out=out, in_=window[:])

@@ -1,6 +1,7 @@
 from contextlib import ExitStack
 
 import concourse.mybir as mybir
+from concourse.masks import make_identity
 
 K, T, S, N = 2048, 1024, 512, 128
 P = 128
@@ -24,14 +25,13 @@ STEPS = (
     ("small", 0, 0, 0, 0, 0),
     ("w", 2, 4, 0, 128, 48),
     ("x", 0, 1, 0, 256, 96),
-    ("x", 1, 2, 0, 256, 112),
+    ("x", 1, 2, 0, 256, 96),
     ("x", 2, 3, 0, 128, 64),
-    ("x", 3, 4, 0, 128, 128),
-    ("x", 2, 3, 128, 256, 56),
-    ("x", 3, 4, 128, 256, 72),
-    ("x", 2, 3, 256, 384, 56),
-    ("gate", 0, 0, 0, 512, 0),
-    ("x", 0, 2, 256, 384, 128),
+    ("x", 3, 4, 0, 128, 64),
+    ("x", 2, 3, 128, 256, 64),
+    ("x", 3, 4, 128, 256, 64),
+    ("x", 0, 1, 256, 384, 64),
+    ("x", 1, 3, 256, 384, 128),
     ("x", 3, 4, 256, 512, 96),
     ("x", 0, 1, 384, 512, 128),
     ("x", 1, 2, 384, 512, 128),
@@ -50,6 +50,7 @@ def tile_picked_place_lin_relu2_sub_l_kernel(tc, xT, w, b, gate, offs, out):
         offsets = keep.tile([P, S // 16], U16, name="offsets")
         bias = keep.tile([P, 1], F32, name="bias")
         gates = keep.tile([P, S], F32, name="gates")
+        gate_row = keep.tile([P, PACK], F32, name="gate_row")
         warm = keep.tile([P, 8], F32, name="warm")
         window = keep.tile([P, T], F32, name="window")
         accs = [psum.tile([P, hi - lo], F32, name=f"acc{lo}") for lo, hi in GROUPS]
@@ -61,8 +62,7 @@ def tile_picked_place_lin_relu2_sub_l_kernel(tc, xT, w, b, gate, offs, out):
             if what == "small":
                 nc.sync.dma_start(offsets[:], offs)
                 nc.sync.dma_start(out=bias[:], in_=b)
-            elif what == "gate":
-                nc.sync.dma_start(out=gates[:, lo:hi], in_=gate[:, lo:hi])
+                nc.sync.dma_start(out=gate_row[:], in_=gate[0].rearrange("(p t) -> p t", t=PACK))
             else:
                 view = w_view if what == "w" else x_view
                 raw = keep.tile([P, c_hi - c_lo, PACK, hi - lo], F32, name=f"raw_{what}{c_lo}_{lo}")
@@ -72,7 +72,13 @@ def tile_picked_place_lin_relu2_sub_l_kernel(tc, xT, w, b, gate, offs, out):
 
         nc.vector.memset(warm[:], 0.0)
         nc.scalar.activation(out=warm[:, 0:1], in_=warm[:, 1:2], func=RELU)
+        identity = keep.tile([P, P], F32, name="identity")
+        make_identity(nc, identity[:])
         nc.gpsimd.memset(window[:], 0.0)
+        spread = psum.tile([P, PACK, P], F32, name="spread")
+        for t in range(PACK):
+            nc.tensor.transpose(spread[:, t, :], gate_row[:, t : t + 1].to_broadcast([P, P]), identity[:])
+        nc.scalar.copy(out=gates[:].rearrange("m (p t) -> m p t", t=PACK), in_=spread[:].rearrange("m t p -> m p t"))
 
         w_parts = {}
         x_parts = {}
@@ -94,7 +100,10 @@ def tile_picked_place_lin_relu2_sub_l_kernel(tc, xT, w, b, gate, offs, out):
                         in_=raw[:, 0, :, a:b].rearrange("p j (s i) -> p s j i", i=4),
                     )
                 else:
-                    copy(out=grouped[:, :, a:b], in_=raw[:, :, :, a:b].rearrange("p c j s -> p c s j"))
+                    copy(
+                        out=grouped[:, :, a:b].rearrange("p c (s i) j -> p c s j i", i=4),
+                        in_=raw[:, :, :, a:b].rearrange("p c j (s i) -> p c s j i", i=4),
+                    )
             nc.vector.quantize_mx(
                 out=codes[:].bitcast(FP8X4), scales=scales[:], in_=grouped[:].rearrange("p c s j -> p (c s j)")
             )
@@ -143,7 +152,7 @@ def tile_picked_place_lin_relu2_sub_l_kernel(tc, xT, w, b, gate, offs, out):
 
         waiting = []
         for n, (what, c_lo, c_hi, lo, hi, share) in enumerate(STEPS):
-            if what in ("small", "gate"):
+            if what == "small":
                 continue
             quantize(n)
             if pending:

@@ -1,13 +1,15 @@
 from contextlib import ExitStack
 
 import concourse.mybir as mybir
-from concourse.masks import make_identity
 
 K, T, S, N = 2048, 1024, 512, 128
 P = 128
 PACK = 4
-K_PASS = P * PACK
-PASSES = K // K_PASS
+PASSES = K // (P * PACK)
+QUARTER = S // 4
+HALF = S // 2
+RUN = 4
+LEAD = 8
 FLOPS = 2 * K * S * N
 
 F32 = mybir.dt.float32
@@ -20,25 +22,21 @@ MULT = mybir.AluOpType.mult
 RELU = mybir.ActivationFunctionType.Relu
 SQUARE = mybir.ActivationFunctionType.Square
 
-STEPS = (
-    ("w", 0, 2, 0, 128, 48),
-    ("small", 0, 0, 0, 0, 0),
-    ("w", 2, 4, 0, 128, 48),
-    ("x", 0, 1, 0, 256, 96),
-    ("x", 1, 2, 0, 256, 96),
-    ("x", 2, 3, 0, 128, 64),
-    ("x", 3, 4, 0, 128, 64),
-    ("x", 2, 3, 128, 256, 64),
-    ("x", 3, 4, 128, 256, 64),
-    ("x", 0, 1, 256, 384, 64),
-    ("x", 1, 3, 256, 384, 128),
-    ("x", 3, 4, 256, 512, 96),
-    ("x", 0, 1, 384, 512, 128),
-    ("x", 1, 2, 384, 512, 128),
-    ("x", 2, 3, 384, 512, 0),
-)
-GROUPS = ((0, 128), (128, 256), (256, 384), (384, 512))
-SCATTER = 128
+WIDE_SHARE = 3
+NARROW_SHARE = 4
+WHOLE = 8
+
+
+def pieces():
+    order = [("w", range(0, 2), 0, N, WIDE_SHARE), ("w", range(2, 4), 0, N, WIDE_SHARE)]
+    order += [("x", range(c, c + 1), 0, HALF, WIDE_SHARE) for c in (0, 1)]
+    order += [("x", range(c, c + 1), q * QUARTER, QUARTER, NARROW_SHARE) for q in (0, 1) for c in (2, 3)]
+    order.append(("x", range(0, 1), 2 * QUARTER, QUARTER, NARROW_SHARE))
+    order.append(("x", range(1, 3), 2 * QUARTER, QUARTER, WHOLE))
+    order.append(("x", range(3, 4), HALF, HALF, WIDE_SHARE))
+    order += [("x", range(c, c + 1), 3 * QUARTER, QUARTER, WHOLE) for c in (0, 1)]
+    order.append(("x", range(2, 3), 3 * QUARTER, QUARTER, 0))
+    return order
 
 
 def tile_picked_place_lin_relu2_sub_l_kernel(tc, xT, w, b, gate, offs, out):
@@ -50,122 +48,99 @@ def tile_picked_place_lin_relu2_sub_l_kernel(tc, xT, w, b, gate, offs, out):
         offsets = keep.tile([P, S // 16], U16, name="offsets")
         bias = keep.tile([P, 1], F32, name="bias")
         gates = keep.tile([P, S], F32, name="gates")
-        gate_row = keep.tile([P, PACK], F32, name="gate_row")
-        warm = keep.tile([P, 8], F32, name="warm")
+        zeros = keep.tile([P, LEAD], F32, name="zeros")
         window = keep.tile([P, T], F32, name="window")
-        accs = [psum.tile([P, hi - lo], F32, name=f"acc{lo}") for lo, hi in GROUPS]
+        accs = [psum.tile([P, QUARTER], F32, name=f"acc{q * QUARTER}") for q in range(S // QUARTER)]
 
-        w_view = w.rearrange("(c p j) n -> c p j n", p=P, j=PACK)
-        x_view = xT.rearrange("(c p j) s -> c p j s", p=P, j=PACK)
-        raws = {}
-        for n, (what, c_lo, c_hi, lo, hi, share) in enumerate(STEPS):
-            if what == "small":
+        views = {
+            "w": w.rearrange("(c p j) n -> c p j n", p=P, j=PACK),
+            "x": xT.rearrange("(c p j) s -> c p j s", p=P, j=PACK),
+        }
+        raws = []
+        for operand, passes, first, width, eighths in pieces():
+            raw = keep.tile([P, len(passes), PACK, width], F32, name=f"raw_{operand}{passes.start}_{first}")
+            for c in passes:
+                nc.sync.dma_start(out=raw[:, c - passes.start], in_=views[operand][c, :, :, first : first + width])
+            raws.append(raw)
+            if operand == "w" and passes.start == 0:
                 nc.sync.dma_start(offsets[:], offs)
                 nc.sync.dma_start(out=bias[:], in_=b)
-                nc.sync.dma_start(out=gate_row[:], in_=gate[0].rearrange("(p t) -> p t", t=PACK))
-            else:
-                view = w_view if what == "w" else x_view
-                raw = keep.tile([P, c_hi - c_lo, PACK, hi - lo], F32, name=f"raw_{what}{c_lo}_{lo}")
-                for c in range(c_lo, c_hi):
-                    nc.sync.dma_start(out=raw[:, c - c_lo], in_=view[c, :, :, lo:hi])
-                raws[n] = raw
+            if first == HALF and passes.start == 0:
+                nc.sync.dma_start(out=gates[:, :HALF], in_=gate[:, :HALF])
+        nc.sync.dma_start(out=gates[:, HALF:], in_=gate[:, HALF:])
 
-        nc.vector.memset(warm[:], 0.0)
-        nc.scalar.activation(out=warm[:, 0:1], in_=warm[:, 1:2], func=RELU)
-        identity = keep.tile([P, P], F32, name="identity")
-        make_identity(nc, identity[:])
-        nc.gpsimd.memset(window[:], 0.0)
-        spread = psum.tile([P, PACK, P], F32, name="spread")
-        for t in range(PACK):
-            nc.tensor.transpose(spread[:, t, :], gate_row[:, t : t + 1].to_broadcast([P, P]), identity[:])
-        nc.scalar.copy(out=gates[:].rearrange("m (p t) -> m p t", t=PACK), in_=spread[:].rearrange("m t p -> m p t"))
+        nc.vector.memset(zeros[:], 0.0)
+        nc.scalar.activation(out=window[:, :LEAD], in_=zeros[:], func=RELU)
+        nc.gpsimd.memset(window[:, LEAD:], 0.0)
 
-        w_parts = {}
-        x_parts = {}
+        quantised = {}
 
-        def quantize(n):
-            what, c_lo, c_hi, lo, hi, share = STEPS[n]
-            raw = raws[n]
-            width = hi - lo
-            passes = c_hi - c_lo
-            grouped = keep.tile([P, passes, width, PACK], BF16, name=f"grouped_{what}{c_lo}_{lo}", align_bytes=64)
-            codes = keep.tile([P, passes * width], U32, name=f"codes_{what}{c_lo}_{lo}", align_bytes=64)
-            scales = keep.tile([P, passes * width], U8, name=f"scales_{what}{c_lo}_{lo}", align_bytes=64)
-            for copy, a, b in ((nc.scalar.copy, 0, share), (nc.vector.tensor_copy, share, width)):
-                if a == b:
+        def quantise(raw, operand, passes, first, width, eighths):
+            name = f"{operand}{passes.start}_{first}"
+            grouped = keep.tile([P, len(passes), width, PACK], BF16, name=f"grouped_{name}", align_bytes=64)
+            codes = keep.tile([P, len(passes) * width], U32, name=f"codes_{name}", align_bytes=64)
+            scales = keep.tile([P, len(passes) * width], U8, name=f"scales_{name}", align_bytes=64)
+            split = width * eighths // 8
+            for copy, lo, hi in ((nc.scalar.copy, 0, split), (nc.vector.tensor_copy, split, width)):
+                if lo == hi:
                     continue
-                if passes == 1:
+                if len(passes) == 1:
                     copy(
-                        out=grouped[:, 0, a:b].rearrange("p (s i) j -> p s j i", i=4),
-                        in_=raw[:, 0, :, a:b].rearrange("p j (s i) -> p s j i", i=4),
+                        out=grouped[:, 0, lo:hi].rearrange("p (s i) j -> p s j i", i=RUN),
+                        in_=raw[:, 0, :, lo:hi].rearrange("p j (s i) -> p s j i", i=RUN),
                     )
                 else:
-                    copy(
-                        out=grouped[:, :, a:b].rearrange("p c (s i) j -> p c s j i", i=4),
-                        in_=raw[:, :, :, a:b].rearrange("p c j (s i) -> p c s j i", i=4),
-                    )
+                    copy(out=grouped[:, :, lo:hi], in_=raw[:, :, :, lo:hi].rearrange("p c j s -> p c s j"))
             nc.vector.quantize_mx(
                 out=codes[:].bitcast(FP8X4), scales=scales[:], in_=grouped[:].rearrange("p c s j -> p (c s j)")
             )
-            for c in range(c_lo, c_hi):
-                part = (codes, scales, (c - c_lo) * width)
-                if what == "w":
-                    w_parts[c] = part
-                else:
-                    x_parts[(c, lo)] = part
+            made = []
+            for c in passes:
+                for at in range(0, width, QUARTER):
+                    cols = slice((c - passes.start) * width + at, (c - passes.start) * width + at + QUARTER)
+                    quantised[(operand, c, (first + at) // QUARTER)] = (codes[:, cols], scales[:, cols])
+                    made.append((c, (first + at) // QUARTER))
+            return made
 
-        products = [0] * len(GROUPS)
+        added = [0] * len(accs)
 
-        def multiply(c, x_lo, g):
-            lo, hi = GROUPS[g]
-            w_codes, w_scales, w_at = w_parts[c]
-            x_codes, x_scales, x_at = x_parts[(c, x_lo)]
-            w_cols = slice(w_at, w_at + N)
-            x_cols = slice(x_at + lo - x_lo, x_at + hi - x_lo)
+        def multiply(c, q):
+            w_codes, w_scales = quantised[("w", c, 0)]
+            x_codes, x_scales = quantised[("x", c, q)]
             nc.tensor.matmul_mx(
-                out=accs[g][:],
-                lhsT=w_codes[:, w_cols].bitcast(FP8X4),
-                lhsT_scale=w_scales[:, w_cols],
-                rhs=x_codes[:, x_cols].bitcast(FP8X4),
-                rhs_scale=x_scales[:, x_cols],
-                start=(products[g] == 0),
-                stop=(products[g] == PASSES - 1),
+                out=accs[q][:],
+                lhsT=w_codes.bitcast(FP8X4),
+                lhsT_scale=w_scales,
+                rhs=x_codes.bitcast(FP8X4),
+                rhs_scale=x_scales,
+                start=(added[q] == 0),
+                stop=(added[q] == PASSES - 1),
             )
-            products[g] += 1
+            added[q] += 1
 
-        pending = []
-
-        def activate(g):
-            lo, hi = GROUPS[g]
-            relu = keep.tile([P, hi - lo], F32, name=f"relu_{lo}")
-            relu2 = keep.tile([P, hi - lo], F32, name=f"relu2_{lo}")
-            nc.scalar.activation(out=relu[:], in_=accs[g][:], func=RELU, bias=bias[:])
+        def activate(q):
+            relu = keep.tile([P, QUARTER], F32, name=f"relu_{q * QUARTER}")
+            relu2 = keep.tile([P, QUARTER], F32, name=f"relu2_{q * QUARTER}")
+            nc.scalar.activation(out=relu[:], in_=accs[q][:], func=RELU, bias=bias[:])
             nc.scalar.activation(out=relu2[:], in_=relu[:], func=SQUARE)
-            for q in range(lo, hi, SCATTER):
-                pending.append((relu2[:, q - lo : q - lo + SCATTER], q, q + SCATTER))
+            return relu2
 
-        def scatter_one():
-            relu2, lo, hi = pending.pop(0)
+        def scatter(q, relu2):
+            lo, hi = q * QUARTER, (q + 1) * QUARTER
             nc.vector.tensor_tensor(
-                window[:].indirect(offsets[:, lo // 16 : hi // 16]), relu2, gates[:, lo:hi], MULT
+                window[:].indirect(offsets[:, lo // 16 : hi // 16]), relu2[:], gates[:, lo:hi], MULT
             )
 
-        waiting = []
-        for n, (what, c_lo, c_hi, lo, hi, share) in enumerate(STEPS):
-            if what == "small":
-                continue
-            quantize(n)
-            if pending:
-                scatter_one()
-            if what == "x":
-                waiting.extend((c, lo, g) for c in range(c_lo, c_hi) for g in range(len(GROUPS)) if lo <= GROUPS[g][0] < hi)
-            ready = [item for item in waiting if item[0] in w_parts]
-            waiting = [item for item in waiting if item[0] not in w_parts]
-            for c, x_lo, g in ready:
-                multiply(c, x_lo, g)
-                if products[g] == PASSES:
-                    activate(g)
-        while pending:
-            scatter_one()
+        finished = []
+        for raw, piece in zip(raws, pieces()):
+            made = quantise(raw, *piece)
+            if finished:
+                scatter(*finished.pop(0))
+            if piece[0] == "x":
+                for c, q in made:
+                    multiply(c, q)
+                    if added[q] == PASSES:
+                        finished.append((q, activate(q)))
+        scatter(*finished.pop(0))
 
         nc.sync.dma_start(out=out, in_=window[:])

@@ -29,8 +29,8 @@ WHOLE = 8
 
 def pieces():
     order = [("w", range(0, 2), 0, N, WIDE_SHARE), ("w", range(2, 4), 0, N, WIDE_SHARE)]
-    order += [("x", range(c, c + 1), 0, HALF, WIDE_SHARE) for c in (0, 1)]
-    order += [("x", range(c, c + 1), q * QUARTER, QUARTER, NARROW_SHARE) for q in (0, 1) for c in (2, 3)]
+    order += [("x", range(c, c + 1), 0, HALF, WIDE_SHARE) for c in (0, 1, 2)]
+    order += [("x", range(3, 4), q * QUARTER, QUARTER, NARROW_SHARE) for q in (0, 1)]
     order.append(("x", range(0, 1), 2 * QUARTER, QUARTER, NARROW_SHARE))
     order.append(("x", range(1, 3), 2 * QUARTER, QUARTER, WHOLE))
     order.append(("x", range(3, 4), HALF, HALF, WIDE_SHARE))
@@ -52,15 +52,16 @@ def tile_picked_place_lin_relu2_sub_l_kernel(tc, xT, w, b, gate, offs, out):
         window = keep.tile([P, T], F32, name="window")
         accs = [psum.tile([P, QUARTER], F32, name=f"acc{q * QUARTER}") for q in range(S // QUARTER)]
 
-        views = {
-            "w": w.rearrange("(c p j) n -> c p j n", p=P, j=PACK),
-            "x": xT.rearrange("(c p j) s -> c p j s", p=P, j=PACK),
-        }
+        w_view = w.rearrange("(c p j) n -> p c j n", p=P, j=PACK)
+        x_view = xT.rearrange("(c p j) s -> c p j s", p=P, j=PACK)
         raws = []
         for operand, passes, first, width, eighths in pieces():
             raw = keep.tile([P, len(passes), PACK, width], F32, name=f"raw_{operand}{passes.start}_{first}")
-            for c in passes:
-                nc.sync.dma_start(out=raw[:, c - passes.start], in_=views[operand][c, :, :, first : first + width])
+            if operand == "w":
+                nc.sync.dma_start(out=raw[:], in_=w_view[:, passes.start : passes.stop])
+            else:
+                for c in passes:
+                    nc.sync.dma_start(out=raw[:, c - passes.start], in_=x_view[c, :, :, first : first + width])
             raws.append(raw)
             if operand == "w" and passes.start == 0:
                 nc.sync.dma_start(offsets[:], offs)

@@ -33,7 +33,7 @@ def pieces():
     order += [("x", range(3, 4), q * QUARTER, QUARTER, NARROW_SHARE) for q in (0, 1)]
     order.append(("x", range(0, 1), 2 * QUARTER, QUARTER, NARROW_SHARE))
     order.append(("x", range(1, 3), 2 * QUARTER, QUARTER, WHOLE))
-    order.append(("x", range(3, 4), HALF, HALF, WIDE_SHARE))
+    order.append(("x", range(3, 4), HALF, HALF, NARROW_SHARE))
     order += [("x", range(c, c + 1), 3 * QUARTER, QUARTER, WHOLE) for c in (0, 1)]
     order.append(("x", range(2, 3), 3 * QUARTER, QUARTER, 0))
     return order
@@ -56,12 +56,13 @@ def tile_picked_place_lin_relu2_sub_l_kernel(tc, xT, w, b, gate, offs, out):
         x_view = xT.rearrange("(c p j) s -> c p j s", p=P, j=PACK)
         raws = []
         for operand, passes, first, width, eighths in pieces():
-            raw = keep.tile([P, len(passes), PACK, width], F32, name=f"raw_{operand}{passes.start}_{first}")
+            shape = [P, len(passes), PACK, width] if operand == "w" else [P, PACK, len(passes), width]
+            raw = keep.tile(shape, F32, name=f"raw_{operand}{passes.start}_{first}")
             if operand == "w":
                 nc.sync.dma_start(out=raw[:], in_=w_view[:, passes.start : passes.stop])
             else:
                 for c in passes:
-                    nc.sync.dma_start(out=raw[:, c - passes.start], in_=x_view[c, :, :, first : first + width])
+                    nc.sync.dma_start(out=raw[:, :, c - passes.start], in_=x_view[c, :, :, first : first + width])
             raws.append(raw)
             if operand == "w" and passes.start == 0:
                 nc.sync.dma_start(offsets[:], offs)
@@ -81,14 +82,15 @@ def tile_picked_place_lin_relu2_sub_l_kernel(tc, xT, w, b, gate, offs, out):
             grouped = keep.tile([P, len(passes), width, PACK], BF16, name=f"grouped_{name}", align_bytes=64)
             codes = keep.tile([P, len(passes) * width], U32, name=f"codes_{name}", align_bytes=64)
             scales = keep.tile([P, len(passes) * width], U8, name=f"scales_{name}", align_bytes=64)
-            split = width * eighths // 8
-            for copy, lo, hi in ((nc.scalar.copy, 0, split), (nc.vector.tensor_copy, split, width)):
+            span = width if operand == "w" else len(passes) * width
+            split = span * eighths // 8
+            for copy, lo, hi in ((nc.scalar.copy, 0, split), (nc.vector.tensor_copy, split, span)):
                 if lo == hi:
                     continue
-                if len(passes) == 1:
+                if operand == "x":
                     copy(
-                        out=grouped[:, 0, lo:hi].rearrange("p (s i) j -> p s j i", i=RUN),
-                        in_=raw[:, 0, :, lo:hi].rearrange("p j (s i) -> p s j i", i=RUN),
+                        out=grouped[:].rearrange("p c s j -> p (c s) j")[:, lo:hi].rearrange("p (s i) j -> p s j i", i=RUN),
+                        in_=raw[:].rearrange("p j c s -> p j (c s)")[:, :, lo:hi].rearrange("p j (s i) -> p s j i", i=RUN),
                     )
                 else:
                     copy(out=grouped[:, :, lo:hi], in_=raw[:, :, :, lo:hi].rearrange("p c j s -> p c s j"))

@@ -27,15 +27,24 @@ NARROW_SHARE = 4
 WHOLE = 8
 
 
-def pieces():
-    order = [("w", range(0, 2), 0, N, WIDE_SHARE), ("w", range(2, 4), 0, N, WIDE_SHARE)]
-    order += [("x", range(c, c + 1), 0, HALF, WIDE_SHARE) for c in (0, 1, 2)]
-    order += [("x", range(3, 4), q * QUARTER, QUARTER, NARROW_SHARE) for q in (0, 1)]
-    order.append(("x", range(0, 1), 2 * QUARTER, QUARTER, NARROW_SHARE))
-    order.append(("x", range(1, 3), 2 * QUARTER, QUARTER, WHOLE))
-    order.append(("x", range(3, 4), HALF, HALF, NARROW_SHARE))
-    order += [("x", range(c, c + 1), 3 * QUARTER, QUARTER, WHOLE) for c in (0, 1)]
-    order.append(("x", range(2, 3), 3 * QUARTER, QUARTER, 0))
+def loads():
+    order = [
+        ("w", range(0, 2), 0, 128, [(0, 128, 3)]),
+        ("w", range(2, 4), 0, 128, [(0, 128, 3)]),
+        ("x", range(0, 1), 0, 256, [(0, 256, 3)]),
+        ("x", range(1, 2), 0, 256, [(0, 256, 3)]),
+        ("x", range(2, 3), 0, 128, [(0, 128, 8)]),
+        ("x", range(3, 4), 0, 128, [(0, 128, 0)]),
+        ("x", range(2, 3), 128, 128, [(0, 128, 8)]),
+        ("x", range(3, 4), 128, 128, [(0, 128, 0)]),
+        ("x", range(0, 1), 256, 128, [(0, 128, 8)]),
+        ("x", range(1, 2), 256, 128, [(0, 128, 0)]),
+        ("x", range(2, 3), 256, 128, [(0, 128, 8)]),
+        ("x", range(3, 4), 256, 256, [(0, 256, 6)]),
+        ("x", range(0, 1), 384, 128, [(0, 128, 8)]),
+        ("x", range(1, 2), 384, 128, [(0, 128, 8)]),
+        ("x", range(2, 3), 384, 128, [(0, 128, 0)]),
+    ]
     return order
 
 
@@ -47,7 +56,7 @@ def tile_picked_place_lin_relu2_sub_l_kernel(tc, xT, w, b, gate, offs, out):
 
         offsets = keep.tile([P, S // 16], U16, name="offsets")
         bias = keep.tile([P, 1], F32, name="bias")
-        gates = keep.tile([P, S], F32, name="gates")
+        gates = keep.tile([P, S], F32, name="gates", align_bytes=64)
         zeros = keep.tile([P, LEAD], F32, name="zeros")
         window = keep.tile([P, T], F32, name="window")
         accs = [psum.tile([P, QUARTER], F32, name=f"acc{q * QUARTER}") for q in range(S // QUARTER)]
@@ -55,19 +64,18 @@ def tile_picked_place_lin_relu2_sub_l_kernel(tc, xT, w, b, gate, offs, out):
         w_view = w.rearrange("(c p j) n -> p c j n", p=P, j=PACK)
         x_view = xT.rearrange("(c p j) s -> c p j s", p=P, j=PACK)
         raws = []
-        for operand, passes, first, width, eighths in pieces():
-            shape = [P, len(passes), PACK, width] if operand == "w" else [P, PACK, len(passes), width]
+        for operand, passes, first, width, parts in loads():
+            shape = [P, len(passes), PACK, width] if operand == "w" else [P, PACK, width]
             raw = keep.tile(shape, F32, name=f"raw_{operand}{passes.start}_{first}")
             if operand == "w":
                 nc.sync.dma_start(out=raw[:], in_=w_view[:, passes.start : passes.stop])
             else:
-                for c in passes:
-                    nc.sync.dma_start(out=raw[:, :, c - passes.start], in_=x_view[c, :, :, first : first + width])
+                nc.sync.dma_start(out=raw[:], in_=x_view[passes.start, :, :, first : first + width])
             raws.append(raw)
             if operand == "w" and passes.start == 0:
                 nc.sync.dma_start(offsets[:], offs)
                 nc.sync.dma_start(out=bias[:], in_=b)
-            if first == HALF and passes.start == 0:
+            if (operand, passes.start, first) == ("x", 3, QUARTER):
                 nc.sync.dma_start(out=gates[:, :HALF], in_=gate[:, :HALF])
         nc.sync.dma_start(out=gates[:, HALF:], in_=gate[:, HALF:])
 
@@ -82,15 +90,14 @@ def tile_picked_place_lin_relu2_sub_l_kernel(tc, xT, w, b, gate, offs, out):
             grouped = keep.tile([P, len(passes), width, PACK], BF16, name=f"grouped_{name}", align_bytes=64)
             codes = keep.tile([P, len(passes) * width], U32, name=f"codes_{name}", align_bytes=64)
             scales = keep.tile([P, len(passes) * width], U8, name=f"scales_{name}", align_bytes=64)
-            span = width if operand == "w" else len(passes) * width
-            split = span * eighths // 8
-            for copy, lo, hi in ((nc.scalar.copy, 0, split), (nc.vector.tensor_copy, split, span)):
+            split = width * eighths // 8
+            for copy, lo, hi in ((nc.scalar.copy, 0, split), (nc.vector.tensor_copy, split, width)):
                 if lo == hi:
                     continue
                 if operand == "x":
                     copy(
-                        out=grouped[:].rearrange("p c s j -> p (c s) j")[:, lo:hi].rearrange("p (s i) j -> p s j i", i=RUN),
-                        in_=raw[:].rearrange("p j c s -> p j (c s)")[:, :, lo:hi].rearrange("p j (s i) -> p s j i", i=RUN),
+                        out=grouped[:, 0, lo:hi].rearrange("p (s i) j -> p s j i", i=RUN),
+                        in_=raw[:, :, lo:hi].rearrange("p j (s i) -> p s j i", i=RUN),
                     )
                 else:
                     copy(out=grouped[:, :, lo:hi], in_=raw[:, :, :, lo:hi].rearrange("p c j s -> p c s j"))
@@ -135,11 +142,14 @@ def tile_picked_place_lin_relu2_sub_l_kernel(tc, xT, w, b, gate, offs, out):
             )
 
         finished = []
-        for raw, piece in zip(raws, pieces()):
-            made = quantise(raw, *piece)
-            if finished:
-                scatter(*finished.pop(0))
-            if piece[0] == "x":
+        for raw, (operand, passes, first, width, parts) in zip(raws, loads()):
+            for at, part_width, eighths in parts:
+                source = raw[:] if operand == "w" else raw[:, :, at : at + part_width]
+                made = quantise(source, operand, passes, first + at, part_width, eighths)
+                if operand == "w":
+                    continue
+                if finished:
+                    scatter(*finished.pop(0))
                 for c, q in made:
                     multiply(c, q)
                     if added[q] == PASSES:

@@ -10,6 +10,7 @@ QUARTER = S // 4
 HALF = S // 2
 RUN = 4
 LEAD = 8
+DMA_ALIGN = 256
 FLOPS = 2 * K * S * N
 
 F32 = mybir.dt.float32
@@ -56,9 +57,9 @@ def tile_picked_place_lin_relu2_sub_l_kernel(tc, xT, w, b, gate, offs, out):
 
         offsets = keep.tile([P, S // 16], U16, name="offsets")
         bias = keep.tile([P, 1], F32, name="bias")
-        gates = keep.tile([P, S], F32, name="gates", align_bytes=64)
+        gates = keep.tile([P, S], F32, name="gates", align_bytes=DMA_ALIGN)
         zeros = keep.tile([P, LEAD], F32, name="zeros")
-        window = keep.tile([P, T], F32, name="window")
+        window = keep.tile([P, T], F32, name="window", align_bytes=DMA_ALIGN)
         accs = [psum.tile([P, QUARTER], F32, name=f"acc{q * QUARTER}") for q in range(S // QUARTER)]
 
         w_view = w.rearrange("(c p j) n -> p c j n", p=P, j=PACK)
@@ -66,7 +67,7 @@ def tile_picked_place_lin_relu2_sub_l_kernel(tc, xT, w, b, gate, offs, out):
         raws = []
         for operand, passes, first, width, parts in loads():
             shape = [P, len(passes), PACK, width] if operand == "w" else [P, PACK, width]
-            raw = keep.tile(shape, F32, name=f"raw_{operand}{passes.start}_{first}")
+            raw = keep.tile(shape, F32, name=f"raw_{operand}{passes.start}_{first}", align_bytes=DMA_ALIGN)
             if operand == "w":
                 nc.sync.dma_start(out=raw[:], in_=w_view[:, passes.start : passes.stop])
             else:

@@ -28,24 +28,15 @@ NARROW_SHARE = 4
 WHOLE = 8
 
 
-def loads():
-    order = [
-        ("w", range(0, 2), 0, 128, [(0, 128, 3)]),
-        ("w", range(2, 4), 0, 128, [(0, 128, 3)]),
-        ("x", range(0, 1), 0, 256, [(0, 256, 3)]),
-        ("x", range(1, 2), 0, 256, [(0, 256, 3)]),
-        ("x", range(2, 3), 0, 128, [(0, 128, 8)]),
-        ("x", range(3, 4), 0, 128, [(0, 128, 0)]),
-        ("x", range(2, 3), 128, 128, [(0, 128, 8)]),
-        ("x", range(3, 4), 128, 128, [(0, 128, 0)]),
-        ("x", range(0, 1), 256, 128, [(0, 128, 8)]),
-        ("x", range(1, 2), 256, 128, [(0, 128, 0)]),
-        ("x", range(2, 3), 256, 128, [(0, 128, 8)]),
-        ("x", range(3, 4), 256, 256, [(0, 256, 6)]),
-        ("x", range(0, 1), 384, 128, [(0, 128, 8)]),
-        ("x", range(1, 2), 384, 128, [(0, 128, 8)]),
-        ("x", range(2, 3), 384, 128, [(0, 128, 0)]),
-    ]
+def pieces():
+    order = [("w", range(0, 2), 0, N, WIDE_SHARE), ("w", range(2, 4), 0, N, WIDE_SHARE)]
+    order += [("x", range(c, c + 1), 0, HALF, WIDE_SHARE) for c in (0, 1)]
+    order += [("x", range(c, c + 1), q * QUARTER, QUARTER, 0 if c == 3 else WHOLE) for q in (0, 1) for c in (2, 3)]
+    order.append(("x", range(0, 1), 2 * QUARTER, QUARTER, WHOLE))
+    order.append(("x", range(1, 3), 2 * QUARTER, QUARTER, WHOLE))
+    order.append(("x", range(3, 4), HALF, HALF, 3))
+    order += [("x", range(c, c + 1), 3 * QUARTER, QUARTER, WHOLE) for c in (0, 1)]
+    order.append(("x", range(2, 3), 3 * QUARTER, QUARTER, 0))
     return order
 
 
@@ -65,18 +56,19 @@ def tile_picked_place_lin_relu2_sub_l_kernel(tc, xT, w, b, gate, offs, out):
         w_view = w.rearrange("(c p j) n -> p c j n", p=P, j=PACK)
         x_view = xT.rearrange("(c p j) s -> c p j s", p=P, j=PACK)
         raws = []
-        for operand, passes, first, width, parts in loads():
-            shape = [P, len(passes), PACK, width] if operand == "w" else [P, PACK, width]
+        for operand, passes, first, width, eighths in pieces():
+            shape = [P, len(passes), PACK, width] if operand == "w" else [P, PACK, len(passes), width]
             raw = keep.tile(shape, F32, name=f"raw_{operand}{passes.start}_{first}", align_bytes=DMA_ALIGN)
             if operand == "w":
                 nc.sync.dma_start(out=raw[:], in_=w_view[:, passes.start : passes.stop])
             else:
-                nc.sync.dma_start(out=raw[:], in_=x_view[passes.start, :, :, first : first + width])
+                for c in passes:
+                    nc.sync.dma_start(out=raw[:, :, c - passes.start], in_=x_view[c, :, :, first : first + width])
             raws.append(raw)
             if operand == "w" and passes.start == 0:
                 nc.sync.dma_start(offsets[:], offs)
                 nc.sync.dma_start(out=bias[:], in_=b)
-            if (operand, passes.start, first) == ("x", 3, QUARTER):
+            if first == QUARTER and passes.start == 3:
                 nc.sync.dma_start(out=gates[:, :HALF], in_=gate[:, :HALF])
         nc.sync.dma_start(out=gates[:, HALF:], in_=gate[:, HALF:])
 
@@ -91,14 +83,15 @@ def tile_picked_place_lin_relu2_sub_l_kernel(tc, xT, w, b, gate, offs, out):
             grouped = keep.tile([P, len(passes), width, PACK], BF16, name=f"grouped_{name}", align_bytes=64)
             codes = keep.tile([P, len(passes) * width], U32, name=f"codes_{name}", align_bytes=64)
             scales = keep.tile([P, len(passes) * width], U8, name=f"scales_{name}", align_bytes=64)
-            split = width * eighths // 8
-            for copy, lo, hi in ((nc.scalar.copy, 0, split), (nc.vector.tensor_copy, split, width)):
+            span = width if operand == "w" else len(passes) * width
+            split = span * eighths // 8
+            for copy, lo, hi in ((nc.scalar.copy, 0, split), (nc.vector.tensor_copy, split, span)):
                 if lo == hi:
                     continue
                 if operand == "x":
                     copy(
-                        out=grouped[:, 0, lo:hi].rearrange("p (s i) j -> p s j i", i=RUN),
-                        in_=raw[:, :, lo:hi].rearrange("p j (s i) -> p s j i", i=RUN),
+                        out=grouped[:].rearrange("p c s j -> p (c s) j")[:, lo:hi].rearrange("p (s i) j -> p s j i", i=RUN),
+                        in_=raw[:].rearrange("p j c s -> p j (c s)")[:, :, lo:hi].rearrange("p j (s i) -> p s j i", i=RUN),
                     )
                 else:
                     copy(out=grouped[:, :, lo:hi], in_=raw[:, :, :, lo:hi].rearrange("p c j s -> p c s j"))
@@ -143,14 +136,11 @@ def tile_picked_place_lin_relu2_sub_l_kernel(tc, xT, w, b, gate, offs, out):
             )
 
         finished = []
-        for raw, (operand, passes, first, width, parts) in zip(raws, loads()):
-            for at, part_width, eighths in parts:
-                source = raw[:] if operand == "w" else raw[:, :, at : at + part_width]
-                made = quantise(source, operand, passes, first + at, part_width, eighths)
-                if operand == "w":
-                    continue
-                if finished:
-                    scatter(*finished.pop(0))
+        for raw, piece in zip(raws, pieces()):
+            made = quantise(raw, *piece)
+            if finished:
+                scatter(*finished.pop(0))
+            if piece[0] == "x":
                 for c, q in made:
                     multiply(c, q)
                     if added[q] == PASSES:

@@ -8,7 +8,7 @@ PACK = 4
 PASSES = K // (P * PACK)
 QUARTER = S // 4
 HALF = S // 2
-RUN = 4
+RUN = 2
 LEAD = 8
 DMA_ALIGN = 256
 FLOPS = 2 * K * S * N

from contextlib import ExitStack

import concourse.mybir as mybir

K, T, S, N = 2048, 1024, 512, 128
P = 128
PACK = 4
PASSES = K // (P * PACK)
QUARTER = S // 4
HALF = S // 2
RUN = 2
LEAD = 8
DMA_ALIGN = 256
FLOPS = 2 * K * S * N

F32 = mybir.dt.float32
BF16 = mybir.dt.bfloat16
U32 = mybir.dt.uint32
U16 = mybir.dt.uint16
U8 = mybir.dt.uint8
FP8X4 = mybir.dt.float8_e4m3fn_x4
MULT = mybir.AluOpType.mult
RELU = mybir.ActivationFunctionType.Relu
SQUARE = mybir.ActivationFunctionType.Square

WIDE_SHARE = 3
NARROW_SHARE = 4
WHOLE = 8


def pieces():
    order = [("w", range(0, 2), 0, N, WIDE_SHARE), ("w", range(2, 4), 0, N, WIDE_SHARE)]
    order += [("x", range(c, c + 1), 0, HALF, WIDE_SHARE) for c in (0, 1)]
    order += [("x", range(c, c + 1), q * QUARTER, QUARTER, 0 if c == 3 else WHOLE) for q in (0, 1) for c in (2, 3)]
    order.append(("x", range(0, 1), 2 * QUARTER, QUARTER, WHOLE))
    order.append(("x", range(1, 3), 2 * QUARTER, QUARTER, WHOLE))
    order.append(("x", range(3, 4), HALF, HALF, 3))
    order += [("x", range(c, c + 1), 3 * QUARTER, QUARTER, WHOLE) for c in (0, 1)]
    order.append(("x", range(2, 3), 3 * QUARTER, QUARTER, 0))
    return order


def tile_picked_place_lin_relu2_sub_l_kernel(tc, xT, w, b, gate, offs, out):
    nc = tc.nc
    with ExitStack() as ctx:
        keep = ctx.enter_context(tc.tile_pool(name="keep", bufs=1))
        psum = ctx.enter_context(tc.psum_pool(name="psum", bufs=1))

        offsets = keep.tile([P, S // 16], U16, name="offsets")
        bias = keep.tile([P, 1], F32, name="bias")
        gates = keep.tile([P, S], F32, name="gates", align_bytes=DMA_ALIGN)
        zeros = keep.tile([P, LEAD], F32, name="zeros")
        window = keep.tile([P, T], F32, name="window", align_bytes=DMA_ALIGN)
        accs = [psum.tile([P, QUARTER], F32, name=f"acc{q * QUARTER}") for q in range(S // QUARTER)]

        w_view = w.rearrange("(c p j) n -> p c j n", p=P, j=PACK)
        x_view = xT.rearrange("(c p j) s -> c p j s", p=P, j=PACK)
        raws = []
        for operand, passes, first, width, eighths in pieces():
            shape = [P, len(passes), PACK, width] if operand == "w" else [P, PACK, len(passes), width]
            raw = keep.tile(shape, F32, name=f"raw_{operand}{passes.start}_{first}", align_bytes=DMA_ALIGN)
            if operand == "w":
                nc.sync.dma_start(out=raw[:], in_=w_view[:, passes.start : passes.stop])
            else:
                for c in passes:
                    nc.sync.dma_start(out=raw[:, :, c - passes.start], in_=x_view[c, :, :, first : first + width])
            raws.append(raw)
            if operand == "w" and passes.start == 0:
                nc.sync.dma_start(offsets[:], offs)
                nc.sync.dma_start(out=bias[:], in_=b)
            if first == QUARTER and passes.start == 3:
                nc.sync.dma_start(out=gates[:, :HALF], in_=gate[:, :HALF])
        nc.sync.dma_start(out=gates[:, HALF:], in_=gate[:, HALF:])

        nc.vector.memset(zeros[:], 0.0)
        nc.scalar.activation(out=window[:, :LEAD], in_=zeros[:], func=RELU)
        nc.gpsimd.memset(window[:, LEAD:], 0.0)

        quantised = {}

        def quantise(raw, operand, passes, first, width, eighths):
            name = f"{operand}{passes.start}_{first}"
            grouped = keep.tile([P, len(passes), width, PACK], BF16, name=f"grouped_{name}", align_bytes=64)
            codes = keep.tile([P, len(passes) * width], U32, name=f"codes_{name}", align_bytes=64)
            scales = keep.tile([P, len(passes) * width], U8, name=f"scales_{name}", align_bytes=64)
            span = width if operand == "w" else len(passes) * width
            split = span * eighths // 8
            for copy, lo, hi in ((nc.scalar.copy, 0, split), (nc.vector.tensor_copy, split, span)):
                if lo == hi:
                    continue
                if operand == "x":
                    copy(
                        out=grouped[:].rearrange("p c s j -> p (c s) j")[:, lo:hi].rearrange("p (s i) j -> p s j i", i=RUN),
                        in_=raw[:].rearrange("p j c s -> p j (c s)")[:, :, lo:hi].rearrange("p j (s i) -> p s j i", i=RUN),
                    )
                else:
                    copy(out=grouped[:, :, lo:hi], in_=raw[:, :, :, lo:hi].rearrange("p c j s -> p c s j"))
            nc.vector.quantize_mx(
                out=codes[:].bitcast(FP8X4), scales=scales[:], in_=grouped[:].rearrange("p c s j -> p (c s j)")
            )
            made = []
            for c in passes:
                for at in range(0, width, QUARTER):
                    cols = slice((c - passes.start) * width + at, (c - passes.start) * width + at + QUARTER)
                    quantised[(operand, c, (first + at) // QUARTER)] = (codes[:, cols], scales[:, cols])
                    made.append((c, (first + at) // QUARTER))
            return made

        added = [0] * len(accs)

        def multiply(c, q):
            w_codes, w_scales = quantised[("w", c, 0)]
            x_codes, x_scales = quantised[("x", c, q)]
            nc.tensor.matmul_mx(
                out=accs[q][:],
                lhsT=w_codes.bitcast(FP8X4),
                lhsT_scale=w_scales,
                rhs=x_codes.bitcast(FP8X4),
                rhs_scale=x_scales,
                start=(added[q] == 0),
                stop=(added[q] == PASSES - 1),
            )
            added[q] += 1

        def activate(q):
            relu = keep.tile([P, QUARTER], F32, name=f"relu_{q * QUARTER}")
            relu2 = keep.tile([P, QUARTER], F32, name=f"relu2_{q * QUARTER}")
            nc.scalar.activation(out=relu[:], in_=accs[q][:], func=RELU, bias=bias[:])
            nc.scalar.activation(out=relu2[:], in_=relu[:], func=SQUARE)
            return relu2

        def scatter(q, relu2):
            lo, hi = q * QUARTER, (q + 1) * QUARTER
            nc.vector.tensor_tensor(
                window[:].indirect(offsets[:, lo // 16 : hi // 16]), relu2[:], gates[:, lo:hi], MULT
            )

        finished = []
        for raw, piece in zip(raws, pieces()):
            made = quantise(raw, *piece)
            if finished:
                scatter(*finished.pop(0))
            if piece[0] == "x":
                for c, q in made:
                    multiply(c, q)
                    if added[q] == PASSES:
                        finished.append((q, activate(q)))
        scatter(*finished.pop(0))

        nc.sync.dma_start(out=out, in_=window[:])
